import numpy as np
import ml_dtypes


def mxq(x, axis, fmt="e4m3"):
    dtype, down = {"e4m3": (ml_dtypes.float8_e4m3fn, 7), "e5m2": (ml_dtypes.float8_e5m2, 14)}[fmt]
    v = np.moveaxis(np.asarray(x, np.float32).astype(ml_dtypes.bfloat16).astype(np.float64), axis, -1)
    blocks = v.reshape(v.shape[:-1] + (-1, 32))
    amax = np.abs(blocks).max(-1, keepdims=True)
    byte = np.maximum(np.where(amax > 0, np.frexp(amax)[1] - 1 + 127, 0) - down, 1)
    scale = np.exp2(byte - 127.0)
    codes = (blocks / scale).astype(np.float32).astype(dtype).astype(np.float64)
    return np.moveaxis((codes * scale).reshape(v.shape), -1, axis)


WIDE = False


def mx_kscale(k):
    if not WIDE:
        return np.ones(k)
    levels = np.array([10, -10, 5, -5, 0])
    if k % 512:
        return np.exp2(np.random.permutation(np.resize(levels, k // 32))).repeat(32)
    a = np.empty((k // 512, 16))
    for p in range(k // 512):
        a[p, :8] = np.random.permutation(np.resize(levels, 8))
        for g in range(8):
            far = levels[np.abs(levels - a[p, g]) >= 10]
            a[p, g + 8] = far[np.random.randint(len(far))]
    return np.exp2(a.ravel()).repeat(32)


def f64(x):
    return np.asarray(x).astype(np.float64)


def striped(idx):
    return np.tile(idx.reshape(-1, 16).T, (8, 1)).astype(np.uint16)


def unstriped(offs):
    return offs[:16].T.reshape(-1).astype(np.int64)


E2M1 = np.array([0.0, 0.5, 1.0, 1.5, 2.0, 3.0, 4.0, 6.0, -0.0, -0.5, -1.0, -1.5, -2.0, -3.0, -4.0, -6.0])


def pack_weight(w, fmt):
    k, n = w.shape
    w = f64(np.asarray(w, np.float32).astype(ml_dtypes.bfloat16)).reshape(k // 32, 32, n)
    amax = np.abs(w).max(1)
    if fmt == "e4m3":
        byte = np.frexp(amax)[1] - 1 + 127 - 7
    else:
        mant, ex = np.frexp(amax / 6.0)
        byte = np.where(mant > 0.5, ex, ex - 1) + 127
    byte = np.clip(np.where(amax > 0, byte, 1), 1, 254)
    scaled = (w * np.exp2(127.0 - byte)[:, None, :]).reshape(k, n).astype(np.float32)
    by_word = np.ascontiguousarray(scaled.reshape(k // 512, 128, 4, n).transpose(0, 1, 3, 2))
    if fmt == "e4m3":
        words = by_word.astype(ml_dtypes.float8_e4m3fn).view(np.uint8)
    else:
        c = by_word.astype(ml_dtypes.float4_e2m1fn).view(np.uint8) & 0xF
        words = (c[..., 0::2] | (c[..., 1::2] << 4)).reshape(k // 512, 128, 2 * n)
    return np.ascontiguousarray(words), np.ascontiguousarray(byte.astype(np.uint8).reshape(k // 512, 16, n))


def unpack_weight(words, scales, fmt):
    g, _, n = scales.shape
    words = np.ascontiguousarray(words).reshape(g, 128, n, -1)
    if fmt == "e4m3":
        vals = words.view(ml_dtypes.float8_e4m3fn).astype(np.float64)
    else:
        nib = np.empty((g, 128, n, 4), np.uint8)
        nib[..., 0::2] = words & 0xF
        nib[..., 1::2] = words >> 4
        vals = E2M1[nib]
    vals = vals * np.repeat(np.exp2(scales.astype(np.float64) - 127.0), 8, axis=1)[..., None]
    return vals.transpose(0, 1, 3, 2).reshape(g * 512, n)


def gelu(v):
    return 0.5 * v * (1.0 + np.tanh(np.sqrt(2.0 / np.pi) * (v + 0.044715 * v**3)))


def bf(x):
    return np.asarray(x, np.float32).astype(ml_dtypes.bfloat16)


def planes(Y):
    n, m = Y.shape
    b = f64(bf(Y)).reshape(n // 32, 32, m)
    amax = np.abs(b).max(1)
    byte = np.clip(np.where(amax > 0, np.frexp(amax)[1] - 1 + 127 - 7, 1), 1, 254)
    codes = (b * np.exp2(127.0 - byte)[:, None, :]).reshape(n, m).astype(np.float32).astype(ml_dtypes.float8_e4m3fn).view(np.uint8)
    words = codes.reshape(n // 512, 128, 4, m).transpose(0, 1, 3, 2)
    return np.ascontiguousarray(words), np.ascontiguousarray(byte.astype(np.uint8).reshape(n // 512, 16, m))


K, T, H, S, T2, P, N = 1536, 4096, 512, 1024, 2048, 1024, 384

def setup_inputs():
    n = np.random.standard_normal
    s = mx_kscale(K)[:, None]
    u = mx_kscale(H)[:, None]
    d = {}
    d["tab_words"], d["tab_scales"] = pack_weight(n((K, T)) * s, "e4m3")
    d["offs"] = striped(np.random.permutation(T)[:S])
    d["offs2"] = striped(np.random.permutation(T2)[:S])
    d["offs3"] = striped(np.random.permutation(T2)[:P])
    d["w1"] = (0.8 * n((K, H)) / K ** 0.5 / s).astype(np.float32)
    d["w2_words"], d["w2_scales"] = pack_weight(0.8 * n((K, H)) / K ** 0.5 / s, "e2m1")
    d["gain"] = (0.8 * np.exp(0.4 * n(H)) * u[:, 0]).astype(np.float32)
    d["page0"] = (n((H, T2)) * u).astype(np.float32)
    d["wgs"] = np.exp(0.3 * n((128, S))).astype(np.float32)
    d["unit"] = (1.5 * np.exp(0.4 * n(H)) / u[:, 0]).astype(np.float32)
    d["level"] = (np.exp(0.4 * n(H)) * u[:, 0]).astype(np.float32)
    d["w3"] = (1.2 * n((H, N)) / H ** 0.5 / u).astype(np.float32)
    return d

def reference(tab_words, tab_scales, offs, offs2, offs3, w1, w2_words, w2_scales,
              gain, page0, wgs, unit, level, w3):
    v = unpack_weight(tab_words, tab_scales, "e4m3")[:, unstriped(offs)]
    left = mxq(f64(w1), 0, "e4m3").T @ v
    right = unpack_weight(w2_words, w2_scales, "e2m1").T @ v
    h = f64(gain)[:, None] * np.square(left - right)
    page = f64(page0).copy()
    page[:, unstriped(offs2)] = np.tile(f64(wgs), (H // 128, 1)) * h
    x = page[:, unstriped(offs3)] * f64(unit)[:, None]
    x = f64(level)[:, None] * np.log(1.0 + np.abs(x))
    y = mxq(f64(w3), 0, "e4m3").T @ mxq(x, 0, "e4m3")
    words, scales = planes(page)
    return y, page, words, scales

@@ -1,0 +1,261 @@
+from contextlib import ExitStack
+
+import concourse.mybir as mybir
+
+K, T, H, S, T2, PM, N = 1536, 4096, 512, 1024, 2048, 1024, 384
+FLOPS = 2 * (2 * K * H * S + H * N * PM)
+
+F32 = mybir.dt.float32
+BF16 = mybir.dt.bfloat16
+I32 = mybir.dt.int32
+U32 = mybir.dt.uint32
+U16 = mybir.dt.uint16
+U8 = mybir.dt.uint8
+FP8X4 = mybir.dt.float8_e4m3fn_x4
+FP4X4 = mybir.dt.float4_e2m1fn_x4
+ACT = mybir.ActivationFunctionType
+MULT = mybir.AluOpType.mult
+
+P = 128
+PACK = 4
+PASSES = K // (P * PACK)
+BANK = 512
+HALVES = 2
+QUADS = 4
+PLANE_CHUNKS = 4
+
+
+def tile_list_toolmark_cell_scores_kernel(
+    tc, tab_words, tab_scales, offs, offs2, offs3, w1, w2_words, w2_scales,
+    gain, page0, wgs, unit, level, w3, out_0, out_1, out_2, out_3,
+):
+    nc = tc.nc
+    with ExitStack() as ctx:
+        lists = ctx.enter_context(tc.tile_pool(name="lists", bufs=1))
+        keep = ctx.enter_context(tc.tile_pool(name="keep", bufs=1))
+        psum = ctx.enter_context(tc.psum_pool(name="psum", bufs=1))
+
+        def sb(shape, dtype, name, tag=None):
+            return keep.tile(shape, dtype, name=name, tag=tag or name, align_bytes=64)
+
+        half_cols = [slice(h * BANK, (h + 1) * BANK) for h in range(HALVES)]
+        half_offs = [slice(h * BANK // 16, (h + 1) * BANK // 16) for h in range(HALVES)]
+
+        one = sb([P, 1], F32, "one")
+        warm = sb([P, 1], F32, "warm")
+        nc.vector.memset(one[:], 1.0)
+        nc.scalar.activation(warm[:], one[:], ACT.Ln)
+
+        tab_s = sb([P, T], U8, "tab_s")
+        w2_s_raw = sb([P, PASSES, H], U8, "w2_s_raw")
+        nc.vector.memset(tab_s[:].bitcast(I32), 0)
+        nc.vector.memset(w2_s_raw[:].bitcast(I32), 0)
+        v_s = [sb([P, S], U8, f"v_s{a}") for a in range(PASSES)]
+        for a in range(1, PASSES):
+            nc.vector.memset(v_s[a][:].bitcast(I32), 0)
+
+        idx = lists.tile([P, S // 16], U16, name="idx")
+        idx2 = lists.tile([P, S // 16], U16, name="idx2")
+        idx3 = lists.tile([P, PM // 16], U16, name="idx3")
+        gain_sb = sb([P, PACK], F32, "gain_sb")
+        unit_sb = sb([P, PACK], F32, "unit_sb")
+        level_sb = sb([P, PACK], F32, "level_sb")
+        w2_raw = sb([P, PASSES, 2 * H], U8, "w2_raw")
+        w1_raw = [sb([P, PACK, H], F32, f"w1_raw{a}", tag=f"mid{a}") for a in range(PASSES)]
+        tab_w = [sb([P, T], I32, f"tab_w{a}", tag=f"big{a}") for a in range(PASSES)]
+
+        def load_w1(a):
+            rows = w1[a * P * PACK : (a + 1) * P * PACK, :]
+            nc.sync.dma_start(w1_raw[a][:], rows.rearrange("(p j) c -> p j c", j=PACK))
+
+        def load_table(a):
+            nc.sync.dma_start(tab_w[a][:], tab_words[a].rearrange("p t i -> p (t i)").bitcast(I32))
+
+        def load_vector(vec_sb, vec):
+            nc.sync.dma_start(vec_sb[:], vec.rearrange("(p t) -> p t", t=PACK))
+
+        nc.sync.dma_start(idx[:], offs)
+        nc.sync.dma_start(w2_raw[:].bitcast(I32), w2_words.rearrange("a p n -> p a n").bitcast(I32))
+        load_w1(0)
+        for q in range(QUADS):
+            nc.sync.dma_start(
+                tab_s[32 * q : 32 * q + 4 * PASSES, :].bitcast(I32),
+                tab_scales[:, 4 * q : 4 * q + 4, :].bitcast(I32),
+            )
+        for q in range(QUADS):
+            nc.sync.dma_start(
+                w2_s_raw[32 * q : 32 * q + 4, :, :].bitcast(I32),
+                w2_scales[:, 4 * q : 4 * q + 4, :].rearrange("a r n -> r a n").bitcast(I32),
+            )
+        load_table(0)
+        load_w1(1)
+        load_table(1)
+        nc.vector.tensor_copy(v_s[0][:], tab_s[:].indirect(idx[:]))
+        for a in range(1, PASSES):
+            nc.sync.dma_start(v_s[a][0:112, :].bitcast(I32), v_s[0][4 * a : 4 * a + 112, :].bitcast(I32))
+        load_w1(2)
+        load_table(2)
+        nc.sync.dma_start(idx2[:], offs2)
+        load_vector(gain_sb, gain)
+        wgs_rows = wgs.rearrange("(q t) j -> q t j", t=PACK)
+        wgs_first = sb([P, S], F32, "wgs_first")
+        for q in range(QUADS):
+            nc.sync.dma_start(wgs_first[32 * q : 32 * q + 32, :], wgs_rows[:, 0, :])
+        page_rows = page0.rearrange("(p t) m -> p t m", t=PACK)
+        page = [sb([P, T2], F32, f"page{t}") for t in range(PACK)]
+        nc.sync.dma_start(page[0][:], page_rows[:, 0, :])
+        nc.sync.dma_start(idx3[:], offs3)
+        load_vector(unit_sb, unit)
+        load_vector(level_sb, level)
+        wgs_rest = sb([P, PACK - 1, S], F32, "wgs_rest")
+        for q in range(QUADS):
+            nc.sync.dma_start(wgs_rest[32 * q : 32 * q + 32, :, :], wgs_rows[:, 1:PACK, :])
+        w3_raw = sb([P, PACK, N], F32, "w3_raw")
+        nc.sync.dma_start(w3_raw[:], w3.rearrange("(p j) n -> p j n", j=PACK))
+        for t in range(1, PACK):
+            nc.sync.dma_start(page[t][:], page_rows[:, t, :])
+        wgs_sb = [wgs_first[:]] + [wgs_rest[:, t, :] for t in range(PACK - 1)]
+
+        w2_c = sb([P, PASSES, 2 * H], U8, "w2_c")
+        w2_s = sb([P, PASSES, H], U8, "w2_s")
+        for a in range(PASSES):
+            nc.vector.tensor_copy(
+                w2_c[:, a, :].rearrange("p (t m b) -> p m t b", t=PACK, b=2),
+                w2_raw[:, a, :].rearrange("p (m t b) -> p m t b", t=PACK, b=2),
+            )
+        nc.vector.tensor_copy(
+            w2_s[:].rearrange("p a (t m) -> p a m t", t=PACK),
+            w2_s_raw[:].rearrange("p a (m t) -> p a m t", t=PACK),
+        )
+
+        acc = [[psum.tile([P, BANK], F32, name=f"acc{t}{h}", tag=f"bank{t}{h}") for h in range(HALVES)] for t in range(PACK)]
+        w1_c = sb([P, PASSES, H], U32, "w1_c")
+        w1_s = sb([P, PASSES, H], U8, "w1_s")
+        for a in range(PASSES):
+            w1_bf = sb([P, PACK * H], BF16, f"w1_bf{a}", tag=f"w1_bf{a % 2}")
+            nc.scalar.activation(
+                w1_bf[:].rearrange("p (t m j) -> p m j t", t=PACK, j=PACK),
+                w1_raw[a][:].rearrange("p j (m t) -> p m j t", t=PACK),
+                ACT.Copy, scale=-1.0,
+            )
+            nc.vector.quantize_mx(out=w1_c[:, a, :].bitcast(FP8X4), scales=w1_s[:, a, :], in_=w1_bf[:])
+            v_w = sb([P, S], U32, f"v_w{a}")
+            for h in range(HALVES):
+                nc.vector.tensor_copy(v_w[:, half_cols[h]], tab_w[a][:].bitcast(U32).indirect(idx[:, half_offs[h]]))
+            for t in range(PACK):
+                for h in range(HALVES):
+                    rhs = v_w[:, half_cols[h]].bitcast(FP8X4)
+                    rhs_scale = v_s[a][:, half_cols[h]]
+                    nc.tensor.matmul_mx(
+                        out=acc[t][h][:],
+                        lhsT=w2_c[:, a, 2 * P * t : 2 * P * (t + 1)].bitcast(FP4X4),
+                        lhsT_scale=w2_s[:, a, P * t : P * (t + 1)],
+                        rhs=rhs, rhs_scale=rhs_scale, start=(a == 0), stop=False,
+                    )
+                    nc.tensor.matmul_mx(
+                        out=acc[t][h][:],
+                        lhsT=w1_c[:, a, P * t : P * (t + 1)].bitcast(FP8X4),
+                        lhsT_scale=w1_s[:, a, P * t : P * (t + 1)],
+                        rhs=rhs, rhs_scale=rhs_scale, start=False, stop=(a == PASSES - 1),
+                    )
+
+        hs = [sb([P, S], F32, f"hs{t}") for t in range(PACK)]
+        nc.vector.tensor_scalar(wgs_first[:], wgs_first[:], gain_sb[:, 0:1], None, MULT)
+        for t in range(PACK):
+            for h in range(HALVES):
+                nc.scalar.activation(hs[t][:, half_cols[h]], acc[t][h][:], ACT.Square)
+            if t > 0:
+                nc.scalar.activation(hs[t][:], hs[t][:], ACT.Copy, scale=gain_sb[:, t : t + 1])
+
+        w3_bf = sb([P, N, PACK], BF16, "w3_bf")
+        w3_s = sb([P, N], U8, "w3_s")
+        nc.scalar.copy(w3_bf[:], w3_raw[:].rearrange("p j n -> p n j"))
+
+        out1_rows = out_1.rearrange("(p t) m -> p t m", t=PACK)
+        pair_lo = sb([P, 2, T2], F32, "pair_lo", tag="big0")
+        width = T2 // PLANE_CHUNKS
+        chunk_cols = [slice(c * width, (c + 1) * width) for c in range(PLANE_CHUNKS)]
+        page_bf = [
+            sb([P, width, PACK], BF16, f"page_bf{c}", tag=("w1_bf0", "w1_bf1", "v_w0", "v_w1")[c])
+            for c in range(PLANE_CHUNKS)
+        ]
+        pair_hi = [
+            sb([P, 2, width], F32, f"pair_hi{c}", tag=("v_w2", "w2_c", "w2_raw", "tab_s")[c])
+            for c in range(PLANE_CHUNKS)
+        ]
+        xg = sb([P, PACK, PM], F32, "xg", tag="big2")
+        x_rows = [[sb([P, 2, BANK], BF16, f"x_rows{u}{h}") for h in range(HALVES)] for u in range(2)]
+        x_bf = [sb([P, BANK, PACK], BF16, f"x_bf{h}", tag=f"mid{h}") for h in range(HALVES)]
+        late = None
+        for t in range(PACK):
+            if t == 0:
+                for h in range(HALVES):
+                    nc.vector.tensor_tensor(
+                        page[t][:].indirect(idx2[:, half_offs[h]]), hs[t][:, half_cols[h]], wgs_sb[t][:, half_cols[h]], MULT
+                    )
+            else:
+                nc.vector.tensor_tensor(page[t][:].indirect(idx2[:]), hs[t][:], wgs_sb[t], MULT)
+            if t < 2:
+                nc.sync.dma_start(pair_lo[:, t, :], page[t][:])
+            else:
+                for c in range(PLANE_CHUNKS):
+                    nc.sync.dma_start(pair_hi[c][:, t - 2, :], page[t][:, chunk_cols[c]])
+            for stored in ((), (0, 1), (2,), (3,))[t]:
+                nc.sync.dma_start(out1_rows[:, stored, :], page[stored][:])
+            for h in range(HALVES):
+                cells = xg[:, t, half_cols[h]]
+                nc.vector.tensor_copy(cells, page[t][:].indirect(idx3[:, half_offs[h]]))
+                logs = cells if t < 2 else late[:, t - 2, half_cols[h]]
+                nc.scalar.activation(logs, cells, ACT.Abs, scale=unit_sb[:, t : t + 1])
+                nc.scalar.activation(logs, logs, ACT.Ln, bias=1.0)
+                nc.scalar.activation(x_rows[t // 2][h][:, t % 2, :], logs, ACT.Copy, scale=level_sb[:, t : t + 1])
+            if t == 2:
+                w3_c = sb([P, N], U32, "w3_c", tag="hs2")
+                for lo, hi in ((0, 256), (256, N)):
+                    nc.vector.quantize_mx(
+                        out=w3_c[:, lo:hi].bitcast(FP8X4), scales=w3_s[:, lo:hi],
+                        in_=w3_bf[:, lo:hi, :].rearrange("p n j -> p (n j)"),
+                    )
+            if t == 1:
+                for h in range(HALVES):
+                    nc.scalar.copy(x_bf[h][:, :, 0:2], x_rows[0][h][:].rearrange("p t m -> p m t"))
+                for c in range(PLANE_CHUNKS):
+                    nc.scalar.copy(page_bf[c][:, :, 0:2], pair_lo[:, :, chunk_cols[c]].rearrange("p t m -> p m t"))
+                late = sb([P, 2, PM], F32, "late", tag="big0")
+
+        x_c = sb([P, PM], U32, "x_c")
+        x_s = sb([P, PM], U8, "x_s")
+        out0_rows = out_0.rearrange("(c p) m -> p c m", p=P)
+        for h in range(HALVES):
+            cols = half_cols[h]
+            nc.vector.tensor_copy(x_bf[h][:, :, 2:4], x_rows[1][h][:].rearrange("p t m -> p m t"))
+            nc.vector.quantize_mx(
+                out=x_c[:, cols].bitcast(FP8X4), scales=x_s[:, cols],
+                in_=x_bf[h][:].rearrange("p m t -> p (m t)"),
+            )
+            y_sb = sb([P, N // P, BANK], F32, f"y_sb{h}", tag=("mid2", "w3_raw")[h])
+            for c in range(N // P):
+                y_ps = psum.tile([P, BANK], F32, name=f"y{c}{h}", tag=f"bank{c}{h}")
+                nc.tensor.matmul_mx(
+                    out=y_ps[:],
+                    lhsT=w3_c[:, P * c : P * (c + 1)].bitcast(FP8X4),
+                    lhsT_scale=w3_s[:, P * c : P * (c + 1)],
+                    rhs=x_c[:, cols].bitcast(FP8X4), rhs_scale=x_s[:, cols],
+                    start=True, stop=True,
+                )
+                nc.scalar.copy(y_sb[:, c, :], y_ps[:])
+            nc.sync.dma_start(out0_rows[:, :, cols], y_sb[:])
+
+        p_s = sb([P, T2], U8, "p_s")
+        words_out = out_2[0].rearrange("p m t -> p (m t)").bitcast(I32)
+        for c in range(PLANE_CHUNKS):
+            cols = chunk_cols[c]
+            p_c = sb([P, width], I32, f"p_c{c}", tag=f"x_rows{1 - c // 2}{c % 2}")
+            nc.vector.tensor_copy(page_bf[c][:, :, 2:4], pair_hi[c][:].rearrange("p t m -> p m t"))
+            nc.vector.quantize_mx(
+                out=p_c[:].bitcast(FP8X4), scales=p_s[:, cols],
+                in_=page_bf[c][:].rearrange("p m t -> p (m t)"),
+            )
+            nc.sync.dma_start(words_out[:, cols], p_c[:])
+        for q in range(QUADS):
+            nc.sync.dma_start(out_3[0, 4 * q : 4 * q + 4, :].bitcast(I32), p_s[32 * q : 32 * q + 4, :].bitcast(I32))

@@ -72,21 +72,26 @@ def tile_list_toolmark_cell_scores_kernel(
             nc.sync.dma_start(tab_w[a][:], tab_words[a].rearrange("p t i -> p (t i)").bitcast(I32))
 
         def load_vector(vec_sb, vec):
-            nc.sync.dma_start(vec_sb[:], vec.rearrange("(p t) -> p t", t=PACK))
+            nc.gpsimd.dma_start(vec_sb[:], vec.rearrange("(p t) -> p t", t=PACK))
 
         nc.sync.dma_start(idx[:], offs)
+        nc.sync.dma_start(idx2[:], offs2)
+        nc.sync.dma_start(idx3[:], offs3)
         nc.sync.dma_start(w2_raw[:].bitcast(I32), w2_words.rearrange("a p n -> p a n").bitcast(I32))
         load_w1(0)
         for q in range(QUADS):
-            nc.sync.dma_start(
+            nc.gpsimd.dma_start(
                 tab_s[32 * q : 32 * q + 4 * PASSES, :].bitcast(I32),
                 tab_scales[:, 4 * q : 4 * q + 4, :].bitcast(I32),
             )
         for q in range(QUADS):
-            nc.sync.dma_start(
+            nc.gpsimd.dma_start(
                 w2_s_raw[32 * q : 32 * q + 4, :, :].bitcast(I32),
                 w2_scales[:, 4 * q : 4 * q + 4, :].rearrange("a r n -> r a n").bitcast(I32),
             )
+        load_vector(gain_sb, gain)
+        load_vector(unit_sb, unit)
+        load_vector(level_sb, level)
         load_table(0)
         load_w1(1)
         load_table(1)
@@ -95,37 +100,34 @@ def tile_list_toolmark_cell_scores_kernel(
             nc.sync.dma_start(v_s[a][0:112, :].bitcast(I32), v_s[0][4 * a : 4 * a + 112, :].bitcast(I32))
         load_w1(2)
         load_table(2)
-        nc.sync.dma_start(idx2[:], offs2)
-        load_vector(gain_sb, gain)
         wgs_rows = wgs.rearrange("(q t) j -> q t j", t=PACK)
-        wgs_first = sb([P, S], F32, "wgs_first")
-        for q in range(QUADS):
-            nc.sync.dma_start(wgs_first[32 * q : 32 * q + 32, :], wgs_rows[:, 0, :])
+        wgs_sb = [sb([P, S], F32, f"wgs_sb{t}") for t in range(PACK)]
+
+        def load_wgs(t, cols):
+            for q in (0, 2, 1, 3):
+                nc.sync.dma_start(wgs_sb[t][32 * q : 32 * q + 32, cols], wgs_rows[:, t, cols])
+
+        load_wgs(0, half_cols[0])
         page_rows = page0.rearrange("(p t) m -> p t m", t=PACK)
         page = [sb([P, T2], F32, f"page{t}") for t in range(PACK)]
         nc.sync.dma_start(page[0][:], page_rows[:, 0, :])
-        nc.sync.dma_start(idx3[:], offs3)
-        load_vector(unit_sb, unit)
-        load_vector(level_sb, level)
-        wgs_rest = sb([P, PACK - 1, S], F32, "wgs_rest")
-        for q in range(QUADS):
-            nc.sync.dma_start(wgs_rest[32 * q : 32 * q + 32, :, :], wgs_rows[:, 1:PACK, :])
+        load_wgs(0, half_cols[1])
         w3_raw = sb([P, PACK, N], F32, "w3_raw")
         nc.sync.dma_start(w3_raw[:], w3.rearrange("(p j) n -> p j n", j=PACK))
         for t in range(1, PACK):
+            load_wgs(t, slice(0, S))
             nc.sync.dma_start(page[t][:], page_rows[:, t, :])
-        wgs_sb = [wgs_first[:]] + [wgs_rest[:, t, :] for t in range(PACK - 1)]
 
         w2_c = sb([P, PASSES, 2 * H], U8, "w2_c")
         w2_s = sb([P, PASSES, H], U8, "w2_s")
         for a in range(PASSES):
             nc.vector.tensor_copy(
-                w2_c[:, a, :].rearrange("p (t m b) -> p m t b", t=PACK, b=2),
-                w2_raw[:, a, :].rearrange("p (m t b) -> p m t b", t=PACK, b=2),
+                w2_c[:, a, :].rearrange("p (t m b) -> p t m b", t=PACK, b=2),
+                w2_raw[:, a, :].rearrange("p (m t b) -> p t m b", t=PACK, b=2),
             )
         nc.vector.tensor_copy(
-            w2_s[:].rearrange("p a (t m) -> p a m t", t=PACK),
-            w2_s_raw[:].rearrange("p a (m t) -> p a m t", t=PACK),
+            w2_s[:].rearrange("p a (t m) -> p a t m", t=PACK),
+            w2_s_raw[:].rearrange("p a (m t) -> p a t m", t=PACK),
         )
 
         acc = [[psum.tile([P, BANK], F32, name=f"acc{t}{h}", tag=f"bank{t}{h}") for h in range(HALVES)] for t in range(PACK)]
@@ -134,8 +136,8 @@ def tile_list_toolmark_cell_scores_kernel(
         for a in range(PASSES):
             w1_bf = sb([P, PACK * H], BF16, f"w1_bf{a}", tag=f"w1_bf{a % 2}")
             nc.scalar.activation(
-                w1_bf[:].rearrange("p (t m j) -> p m j t", t=PACK, j=PACK),
-                w1_raw[a][:].rearrange("p j (m t) -> p m j t", t=PACK),
+                w1_bf[:].rearrange("p (t m j) -> p t m j", t=PACK, j=PACK),
+                w1_raw[a][:].rearrange("p j (m t) -> p t m j", t=PACK),
                 ACT.Copy, scale=-1.0,
             )
             nc.vector.quantize_mx(out=w1_c[:, a, :].bitcast(FP8X4), scales=w1_s[:, a, :], in_=w1_bf[:])
@@ -160,7 +162,6 @@ def tile_list_toolmark_cell_scores_kernel(
                     )
 
         hs = [sb([P, S], F32, f"hs{t}") for t in range(PACK)]
-        nc.vector.tensor_scalar(wgs_first[:], wgs_first[:], gain_sb[:, 0:1], None, MULT)
         for t in range(PACK):
             for h in range(HALVES):
                 nc.scalar.activation(hs[t][:, half_cols[h]], acc[t][h][:], ACT.Square)
@@ -184,17 +185,19 @@ def tile_list_toolmark_cell_scores_kernel(
             for c in range(PLANE_CHUNKS)
         ]
         xg = sb([P, PACK, PM], F32, "xg", tag="big2")
-        x_rows = [[sb([P, 2, BANK], BF16, f"x_rows{u}{h}") for h in range(HALVES)] for u in range(2)]
+        x_rows = [sb([P, 2, BANK], BF16, f"x_rows{h}") for h in range(HALVES)]
         x_bf = [sb([P, BANK, PACK], BF16, f"x_bf{h}", tag=f"mid{h}") for h in range(HALVES)]
         late = None
         for t in range(PACK):
             if t == 0:
                 for h in range(HALVES):
+                    first = wgs_sb[0][:, half_cols[h]]
+                    nc.vector.tensor_scalar(first, first, gain_sb[:, 0:1], None, MULT)
                     nc.vector.tensor_tensor(
                         page[t][:].indirect(idx2[:, half_offs[h]]), hs[t][:, half_cols[h]], wgs_sb[t][:, half_cols[h]], MULT
                     )
             else:
-                nc.vector.tensor_tensor(page[t][:].indirect(idx2[:]), hs[t][:], wgs_sb[t], MULT)
+                nc.vector.tensor_tensor(page[t][:].indirect(idx2[:]), hs[t][:], wgs_sb[t][:], MULT)
             if t < 2:
                 nc.sync.dma_start(pair_lo[:, t, :], page[t][:])
             else:
@@ -208,7 +211,8 @@ def tile_list_toolmark_cell_scores_kernel(
                 logs = cells if t < 2 else late[:, t - 2, half_cols[h]]
                 nc.scalar.activation(logs, cells, ACT.Abs, scale=unit_sb[:, t : t + 1])
                 nc.scalar.activation(logs, logs, ACT.Ln, bias=1.0)
-                nc.scalar.activation(x_rows[t // 2][h][:, t % 2, :], logs, ACT.Copy, scale=level_sb[:, t : t + 1])
+                rounded = x_bf[h][:, :, t] if t < 2 else x_rows[h][:, t - 2, :]
+                nc.scalar.activation(rounded, logs, ACT.Copy, scale=level_sb[:, t : t + 1])
             if t == 2:
                 w3_c = sb([P, N], U32, "w3_c", tag="hs2")
                 for lo, hi in ((0, 256), (256, N)):
@@ -217,8 +221,6 @@ def tile_list_toolmark_cell_scores_kernel(
                         in_=w3_bf[:, lo:hi, :].rearrange("p n j -> p (n j)"),
                     )
             if t == 1:
-                for h in range(HALVES):
-                    nc.scalar.copy(x_bf[h][:, :, 0:2], x_rows[0][h][:].rearrange("p t m -> p m t"))
                 for c in range(PLANE_CHUNKS):
                     nc.scalar.copy(page_bf[c][:, :, 0:2], pair_lo[:, :, chunk_cols[c]].rearrange("p t m -> p m t"))
                 late = sb([P, 2, PM], F32, "late", tag="big0")
@@ -228,7 +230,7 @@ def tile_list_toolmark_cell_scores_kernel(
         out0_rows = out_0.rearrange("(c p) m -> p c m", p=P)
         for h in range(HALVES):
             cols = half_cols[h]
-            nc.vector.tensor_copy(x_bf[h][:, :, 2:4], x_rows[1][h][:].rearrange("p t m -> p m t"))
+            nc.vector.tensor_copy(x_bf[h][:, :, 2:4], x_rows[h][:].rearrange("p t m -> p m t"))
             nc.vector.quantize_mx(
                 out=x_c[:, cols].bitcast(FP8X4), scales=x_s[:, cols],
                 in_=x_bf[h][:].rearrange("p m t -> p (m t)"),
@@ -250,7 +252,7 @@ def tile_list_toolmark_cell_scores_kernel(
         words_out = out_2[0].rearrange("p m t -> p (m t)").bitcast(I32)
         for c in range(PLANE_CHUNKS):
             cols = chunk_cols[c]
-            p_c = sb([P, width], I32, f"p_c{c}", tag=f"x_rows{1 - c // 2}{c % 2}")
+            p_c = sb([P, width], I32, f"p_c{c}", tag=("x_rows0", "x_rows1", "p_c2", "p_c3")[c])
             nc.vector.tensor_copy(page_bf[c][:, :, 2:4], pair_hi[c][:].rearrange("p t m -> p m t"))
             nc.vector.quantize_mx(
                 out=p_c[:].bitcast(FP8X4), scales=p_s[:, cols],

@@ -72,51 +72,54 @@ def tile_list_toolmark_cell_scores_kernel(
             nc.sync.dma_start(tab_w[a][:], tab_words[a].rearrange("p t i -> p (t i)").bitcast(I32))
 
         def load_vector(vec_sb, vec):
-            nc.gpsimd.dma_start(vec_sb[:], vec.rearrange("(p t) -> p t", t=PACK))
+            nc.sync.dma_start(vec_sb[:], vec.rearrange("(p t) -> p t", t=PACK))
 
         nc.sync.dma_start(idx[:], offs)
-        nc.sync.dma_start(idx2[:], offs2)
-        nc.sync.dma_start(idx3[:], offs3)
         nc.sync.dma_start(w2_raw[:].bitcast(I32), w2_words.rearrange("a p n -> p a n").bitcast(I32))
         load_w1(0)
         for q in range(QUADS):
-            nc.gpsimd.dma_start(
+            nc.sync.dma_start(
                 tab_s[32 * q : 32 * q + 4 * PASSES, :].bitcast(I32),
                 tab_scales[:, 4 * q : 4 * q + 4, :].bitcast(I32),
             )
         for q in range(QUADS):
-            nc.gpsimd.dma_start(
+            nc.sync.dma_start(
                 w2_s_raw[32 * q : 32 * q + 4, :, :].bitcast(I32),
                 w2_scales[:, 4 * q : 4 * q + 4, :].rearrange("a r n -> r a n").bitcast(I32),
             )
-        load_vector(gain_sb, gain)
-        load_vector(unit_sb, unit)
-        load_vector(level_sb, level)
         load_table(0)
         load_w1(1)
         load_table(1)
         nc.vector.tensor_copy(v_s[0][:], tab_s[:].indirect(idx[:]))
         for a in range(1, PASSES):
             nc.sync.dma_start(v_s[a][0:112, :].bitcast(I32), v_s[0][4 * a : 4 * a + 112, :].bitcast(I32))
-        load_w1(2)
+        nc.sync.dma_start(idx2[:], offs2)
+        load_vector(gain_sb, gain)
         load_table(2)
+        load_w1(2)
         wgs_rows = wgs.rearrange("(q t) j -> q t j", t=PACK)
         wgs_sb = [sb([P, S], F32, f"wgs_sb{t}") for t in range(PACK)]
+        page_rows = page0.rearrange("(p t) m -> p t m", t=PACK)
+        page = [sb([P, T2], F32, f"page{t}") for t in range(PACK)]
 
         def load_wgs(t, cols):
             for q in (0, 2, 1, 3):
                 nc.sync.dma_start(wgs_sb[t][32 * q : 32 * q + 32, cols], wgs_rows[:, t, cols])
 
+        def load_slice(t):
+            load_wgs(t, slice(0, S))
+            nc.sync.dma_start(page[t][:], page_rows[:, t, :])
+
         load_wgs(0, half_cols[0])
-        page_rows = page0.rearrange("(p t) m -> p t m", t=PACK)
-        page = [sb([P, T2], F32, f"page{t}") for t in range(PACK)]
         nc.sync.dma_start(page[0][:], page_rows[:, 0, :])
         load_wgs(0, half_cols[1])
+        nc.sync.dma_start(idx3[:], offs3)
+        load_vector(unit_sb, unit)
+        load_vector(level_sb, level)
         w3_raw = sb([P, PACK, N], F32, "w3_raw")
         nc.sync.dma_start(w3_raw[:], w3.rearrange("(p j) n -> p j n", j=PACK))
         for t in range(1, PACK):
-            load_wgs(t, slice(0, S))
-            nc.sync.dma_start(page[t][:], page_rows[:, t, :])
+            load_slice(t)
 
         w2_c = sb([P, PASSES, 2 * H], U8, "w2_c")
         w2_s = sb([P, PASSES, H], U8, "w2_s")
@@ -130,41 +133,47 @@ def tile_list_toolmark_cell_scores_kernel(
             w2_s_raw[:].rearrange("p a (m t) -> p a t m", t=PACK),
         )
 
-        acc = [[psum.tile([P, BANK], F32, name=f"acc{t}{h}", tag=f"bank{t}{h}") for h in range(HALVES)] for t in range(PACK)]
         w1_c = sb([P, PASSES, H], U32, "w1_c")
         w1_s = sb([P, PASSES, H], U8, "w1_s")
+        v_w = [sb([P, S], U32, f"v_w{a}") for a in range(PASSES)]
         for a in range(PASSES):
             w1_bf = sb([P, PACK * H], BF16, f"w1_bf{a}", tag=f"w1_bf{a % 2}")
-            nc.scalar.activation(
-                w1_bf[:].rearrange("p (t m j) -> p t m j", t=PACK, j=PACK),
-                w1_raw[a][:].rearrange("p j (m t) -> p t m j", t=PACK),
-                ACT.Copy, scale=-1.0,
-            )
-            nc.vector.quantize_mx(out=w1_c[:, a, :].bitcast(FP8X4), scales=w1_s[:, a, :], in_=w1_bf[:])
-            v_w = sb([P, S], U32, f"v_w{a}")
+            dealt = w1_bf[:].rearrange("p (t m j) -> p m j t", t=PACK, j=PACK)
+            raw = w1_raw[a][:].rearrange("p j (m t) -> p m j t", t=PACK)
             for h in range(HALVES):
-                nc.vector.tensor_copy(v_w[:, half_cols[h]], tab_w[a][:].bitcast(U32).indirect(idx[:, half_offs[h]]))
-            for t in range(PACK):
-                for h in range(HALVES):
-                    rhs = v_w[:, half_cols[h]].bitcast(FP8X4)
+                nc.vector.tensor_copy(v_w[a][:, half_cols[h]], tab_w[a][:].bitcast(U32).indirect(idx[:, half_offs[h]]))
+            if a < PASSES - 1:
+                nc.scalar.activation(dealt, raw, ACT.Copy, scale=-1.0)
+                spans = [(0, H)]
+            else:
+                nc.vector.tensor_scalar(dealt[:, :, :, 0], raw[:, :, :, 0], -1.0, None, MULT)
+                nc.scalar.activation(dealt[:, :, :, 1:PACK], raw[:, :, :, 1:PACK], ACT.Copy, scale=-1.0)
+                spans = [(0, P), (P, 2 * P), (2 * P, H)]
+            for lo, hi in spans:
+                nc.vector.quantize_mx(
+                    out=w1_c[:, a, lo:hi].bitcast(FP8X4), scales=w1_s[:, a, lo:hi], in_=w1_bf[:, PACK * lo : PACK * hi]
+                )
+
+        hs = [sb([P, S], F32, f"hs{t}") for t in range(PACK)]
+        for t in range(PACK):
+            for h in range(HALVES):
+                acc = psum.tile([P, BANK], F32, name=f"acc{t}{h}", tag=f"bank{t % 2}{h}")
+                for a in range(PASSES):
+                    rhs = v_w[a][:, half_cols[h]].bitcast(FP8X4)
                     rhs_scale = v_s[a][:, half_cols[h]]
                     nc.tensor.matmul_mx(
-                        out=acc[t][h][:],
+                        out=acc[:],
                         lhsT=w2_c[:, a, 2 * P * t : 2 * P * (t + 1)].bitcast(FP4X4),
                         lhsT_scale=w2_s[:, a, P * t : P * (t + 1)],
                         rhs=rhs, rhs_scale=rhs_scale, start=(a == 0), stop=False,
                     )
                     nc.tensor.matmul_mx(
-                        out=acc[t][h][:],
+                        out=acc[:],
                         lhsT=w1_c[:, a, P * t : P * (t + 1)].bitcast(FP8X4),
                         lhsT_scale=w1_s[:, a, P * t : P * (t + 1)],
                         rhs=rhs, rhs_scale=rhs_scale, start=False, stop=(a == PASSES - 1),
                     )
-
-        hs = [sb([P, S], F32, f"hs{t}") for t in range(PACK)]
-        for t in range(PACK):
-            for h in range(HALVES):
-                nc.scalar.activation(hs[t][:, half_cols[h]], acc[t][h][:], ACT.Square)
+                nc.scalar.activation(hs[t][:, half_cols[h]], acc[:], ACT.Square)
             if t > 0:
                 nc.scalar.activation(hs[t][:], hs[t][:], ACT.Copy, scale=gain_sb[:, t : t + 1])
 
@@ -173,71 +182,65 @@ def tile_list_toolmark_cell_scores_kernel(
         nc.scalar.copy(w3_bf[:], w3_raw[:].rearrange("p j n -> p n j"))
 
         out1_rows = out_1.rearrange("(p t) m -> p t m", t=PACK)
-        pair_lo = sb([P, 2, T2], F32, "pair_lo", tag="big0")
         width = T2 // PLANE_CHUNKS
         chunk_cols = [slice(c * width, (c + 1) * width) for c in range(PLANE_CHUNKS)]
-        page_bf = [
-            sb([P, width, PACK], BF16, f"page_bf{c}", tag=("w1_bf0", "w1_bf1", "v_w0", "v_w1")[c])
-            for c in range(PLANE_CHUNKS)
-        ]
-        pair_hi = [
-            sb([P, 2, width], F32, f"pair_hi{c}", tag=("v_w2", "w2_c", "w2_raw", "tab_s")[c])
+        rows4 = [
+            sb([P, PACK, width], F32, f"rows4_{c}", tag=("big0", "big1", "rows4_2", "rows4_3")[c])
             for c in range(PLANE_CHUNKS)
         ]
         xg = sb([P, PACK, PM], F32, "xg", tag="big2")
-        x_rows = [sb([P, 2, BANK], BF16, f"x_rows{h}") for h in range(HALVES)]
+        x_rows = [sb([P, PACK, BANK], BF16, f"x_rows{h}") for h in range(HALVES)]
         x_bf = [sb([P, BANK, PACK], BF16, f"x_bf{h}", tag=f"mid{h}") for h in range(HALVES)]
-        late = None
+        size_last = sb([P, BANK], F32, "size_last")
+        last = PACK - 1
         for t in range(PACK):
             if t == 0:
                 for h in range(HALVES):
                     first = wgs_sb[0][:, half_cols[h]]
                     nc.vector.tensor_scalar(first, first, gain_sb[:, 0:1], None, MULT)
                     nc.vector.tensor_tensor(
-                        page[t][:].indirect(idx2[:, half_offs[h]]), hs[t][:, half_cols[h]], wgs_sb[t][:, half_cols[h]], MULT
+                        page[t][:].indirect(idx2[:, half_offs[h]]), hs[t][:, half_cols[h]], first, MULT
                     )
             else:
                 nc.vector.tensor_tensor(page[t][:].indirect(idx2[:]), hs[t][:], wgs_sb[t][:], MULT)
-            if t < 2:
-                nc.sync.dma_start(pair_lo[:, t, :], page[t][:])
-            else:
-                for c in range(PLANE_CHUNKS):
-                    nc.sync.dma_start(pair_hi[c][:, t - 2, :], page[t][:, chunk_cols[c]])
-            for stored in ((), (0, 1), (2,), (3,))[t]:
-                nc.sync.dma_start(out1_rows[:, stored, :], page[stored][:])
-            for h in range(HALVES):
-                cells = xg[:, t, half_cols[h]]
-                nc.vector.tensor_copy(cells, page[t][:].indirect(idx3[:, half_offs[h]]))
-                logs = cells if t < 2 else late[:, t - 2, half_cols[h]]
-                nc.scalar.activation(logs, cells, ACT.Abs, scale=unit_sb[:, t : t + 1])
-                nc.scalar.activation(logs, logs, ACT.Ln, bias=1.0)
-                rounded = x_bf[h][:, :, t] if t < 2 else x_rows[h][:, t - 2, :]
-                nc.scalar.activation(rounded, logs, ACT.Copy, scale=level_sb[:, t : t + 1])
-            if t == 2:
-                w3_c = sb([P, N], U32, "w3_c", tag="hs2")
-                for lo, hi in ((0, 256), (256, N)):
-                    nc.vector.quantize_mx(
-                        out=w3_c[:, lo:hi].bitcast(FP8X4), scales=w3_s[:, lo:hi],
-                        in_=w3_bf[:, lo:hi, :].rearrange("p n j -> p (n j)"),
+            for c in (3, 0, 1, 2):
+                if t < last:
+                    nc.scalar.copy(rows4[c][:, t, :], page[t][:, chunk_cols[c]])
+                else:
+                    nc.sync.dma_start(rows4[c][:, t, :], page[t][:, chunk_cols[c]])
+            nc.sync.dma_start(out1_rows[:, t, :], page[t][:])
+            pieces = [range(HALVES)] if t < last else [range(h, h + 1) for h in range(HALVES)]
+            for halves in pieces:
+                cols = slice(halves.start * BANK, halves.stop * BANK)
+                cells = xg[:, t, cols]
+                nc.vector.tensor_copy(cells, page[t][:].indirect(idx3[:, cols.start // 16 : cols.stop // 16]))
+                size = cells if t < last else size_last[:]
+                nc.scalar.activation(size, cells, ACT.Abs, scale=unit_sb[:, t : t + 1])
+                nc.scalar.activation(cells, size, ACT.Ln, bias=1.0)
+                for h in halves:
+                    nc.scalar.activation(
+                        x_rows[h][:, t, :], xg[:, t, half_cols[h]], ACT.Copy, scale=level_sb[:, t : t + 1]
                     )
-            if t == 1:
-                for c in range(PLANE_CHUNKS):
-                    nc.scalar.copy(page_bf[c][:, :, 0:2], pair_lo[:, :, chunk_cols[c]].rearrange("p t m -> p m t"))
-                late = sb([P, 2, PM], F32, "late", tag="big0")
+        w3_c = sb([P, N], U32, "w3_c", tag="hs3")
+        for lo, hi in ((0, 256), (256, N)):
+            nc.vector.quantize_mx(
+                out=w3_c[:, lo:hi].bitcast(FP8X4), scales=w3_s[:, lo:hi],
+                in_=w3_bf[:, lo:hi, :].rearrange("p n j -> p (n j)"),
+            )
 
         x_c = sb([P, PM], U32, "x_c")
         x_s = sb([P, PM], U8, "x_s")
         out0_rows = out_0.rearrange("(c p) m -> p c m", p=P)
         for h in range(HALVES):
             cols = half_cols[h]
-            nc.vector.tensor_copy(x_bf[h][:, :, 2:4], x_rows[h][:].rearrange("p t m -> p m t"))
+            nc.vector.tensor_copy(x_bf[h][:], x_rows[h][:].rearrange("p t m -> p m t"))
             nc.vector.quantize_mx(
                 out=x_c[:, cols].bitcast(FP8X4), scales=x_s[:, cols],
                 in_=x_bf[h][:].rearrange("p m t -> p (m t)"),
             )
             y_sb = sb([P, N // P, BANK], F32, f"y_sb{h}", tag=("mid2", "w3_raw")[h])
             for c in range(N // P):
-                y_ps = psum.tile([P, BANK], F32, name=f"y{c}{h}", tag=f"bank{c}{h}")
+                y_ps = psum.tile([P, BANK], F32, name=f"y{c}{h}", tag=f"score{c}{h}" if c else f"bank0{h}")
                 nc.tensor.matmul_mx(
                     out=y_ps[:],
                     lhsT=w3_c[:, P * c : P * (c + 1)].bitcast(FP8X4),
@@ -246,17 +249,21 @@ def tile_list_toolmark_cell_scores_kernel(
                     start=True, stop=True,
                 )
                 nc.scalar.copy(y_sb[:, c, :], y_ps[:])
-            nc.sync.dma_start(out0_rows[:, :, cols], y_sb[:])
+                nc.sync.dma_start(out0_rows[:, c, cols], y_sb[:, c, :])
 
         p_s = sb([P, T2], U8, "p_s")
         words_out = out_2[0].rearrange("p m t -> p (m t)").bitcast(I32)
         for c in range(PLANE_CHUNKS):
             cols = chunk_cols[c]
-            p_c = sb([P, width], I32, f"p_c{c}", tag=("x_rows0", "x_rows1", "p_c2", "p_c3")[c])
-            nc.vector.tensor_copy(page_bf[c][:, :, 2:4], pair_hi[c][:].rearrange("p t m -> p m t"))
+            p_c = sb([P, width], I32, f"p_c{c}")
+            page_bf = sb([P, width, PACK], BF16, f"page_bf{c}", tag=("x_rows0", "x_rows1", "mid1", "page_bf3")[c])
+            if c < PLANE_CHUNKS - 1:
+                nc.vector.tensor_copy(page_bf[:], rows4[c][:].rearrange("p t m -> p m t"))
+            else:
+                nc.scalar.copy(page_bf[:], rows4[c][:].rearrange("p t m -> p m t"))
             nc.vector.quantize_mx(
                 out=p_c[:].bitcast(FP8X4), scales=p_s[:, cols],
-                in_=page_bf[c][:].rearrange("p m t -> p (m t)"),
+                in_=page_bf[:].rearrange("p m t -> p (m t)"),
             )
             nc.sync.dma_start(words_out[:, cols], p_c[:])
         for q in range(QUADS):

from contextlib import ExitStack

import concourse.mybir as mybir

K, T, H, S, T2, PM, N = 1536, 4096, 512, 1024, 2048, 1024, 384
FLOPS = 2 * (2 * K * H * S + H * N * PM)

F32 = mybir.dt.float32
BF16 = mybir.dt.bfloat16
I32 = mybir.dt.int32
U32 = mybir.dt.uint32
U16 = mybir.dt.uint16
U8 = mybir.dt.uint8
FP8X4 = mybir.dt.float8_e4m3fn_x4
FP4X4 = mybir.dt.float4_e2m1fn_x4
ACT = mybir.ActivationFunctionType
MULT = mybir.AluOpType.mult

P = 128
PACK = 4
PASSES = K // (P * PACK)
BANK = 512
HALVES = 2
QUADS = 4
PLANE_CHUNKS = 4


def tile_list_toolmark_cell_scores_kernel(
    tc, tab_words, tab_scales, offs, offs2, offs3, w1, w2_words, w2_scales,
    gain, page0, wgs, unit, level, w3, out_0, out_1, out_2, out_3,
):
    nc = tc.nc
    with ExitStack() as ctx:
        lists = ctx.enter_context(tc.tile_pool(name="lists", bufs=1))
        keep = ctx.enter_context(tc.tile_pool(name="keep", bufs=1))
        psum = ctx.enter_context(tc.psum_pool(name="psum", bufs=1))

        def sb(shape, dtype, name, tag=None):
            return keep.tile(shape, dtype, name=name, tag=tag or name, align_bytes=64)

        half_cols = [slice(h * BANK, (h + 1) * BANK) for h in range(HALVES)]
        half_offs = [slice(h * BANK // 16, (h + 1) * BANK // 16) for h in range(HALVES)]

        one = sb([P, 1], F32, "one")
        warm = sb([P, 1], F32, "warm")
        nc.vector.memset(one[:], 1.0)
        nc.scalar.activation(warm[:], one[:], ACT.Ln)

        tab_s = sb([P, T], U8, "tab_s")
        w2_s_raw = sb([P, PASSES, H], U8, "w2_s_raw")
        nc.vector.memset(tab_s[:].bitcast(I32), 0)
        nc.vector.memset(w2_s_raw[:].bitcast(I32), 0)
        v_s = [sb([P, S], U8, f"v_s{a}") for a in range(PASSES)]
        for a in range(1, PASSES):
            nc.vector.memset(v_s[a][:].bitcast(I32), 0)

        idx = lists.tile([P, S // 16], U16, name="idx")
        idx2 = lists.tile([P, S // 16], U16, name="idx2")
        idx3 = lists.tile([P, PM // 16], U16, name="idx3")
        gain_sb = sb([P, PACK], F32, "gain_sb")
        unit_sb = sb([P, PACK], F32, "unit_sb")
        level_sb = sb([P, PACK], F32, "level_sb")
        w2_raw = sb([P, PASSES, 2 * H], U8, "w2_raw")
        w1_raw = [sb([P, PACK, H], F32, f"w1_raw{a}", tag=f"mid{a}") for a in range(PASSES)]
        tab_w = [sb([P, T], I32, f"tab_w{a}", tag=f"big{a}") for a in range(PASSES)]

        def load_w1(a):
            rows = w1[a * P * PACK : (a + 1) * P * PACK, :]
            nc.sync.dma_start(w1_raw[a][:], rows.rearrange("(p j) c -> p j c", j=PACK))

        def load_table(a):
            nc.sync.dma_start(tab_w[a][:], tab_words[a].rearrange("p t i -> p (t i)").bitcast(I32))

        def load_vector(vec_sb, vec):
            nc.sync.dma_start(vec_sb[:], vec.rearrange("(p t) -> p t", t=PACK))

        nc.sync.dma_start(idx[:], offs)
        nc.sync.dma_start(w2_raw[:].bitcast(I32), w2_words.rearrange("a p n -> p a n").bitcast(I32))
        load_w1(0)
        for q in range(QUADS):
            nc.sync.dma_start(
                tab_s[32 * q : 32 * q + 4 * PASSES, :].bitcast(I32),
                tab_scales[:, 4 * q : 4 * q + 4, :].bitcast(I32),
            )
        for q in range(QUADS):
            nc.sync.dma_start(
                w2_s_raw[32 * q : 32 * q + 4, :, :].bitcast(I32),
                w2_scales[:, 4 * q : 4 * q + 4, :].rearrange("a r n -> r a n").bitcast(I32),
            )
        load_table(0)
        load_w1(1)
        load_table(1)
        nc.vector.tensor_copy(v_s[0][:], tab_s[:].indirect(idx[:]))
        for a in range(1, PASSES):
            nc.sync.dma_start(v_s[a][0:112, :].bitcast(I32), v_s[0][4 * a : 4 * a + 112, :].bitcast(I32))
        nc.sync.dma_start(idx2[:], offs2)
        load_vector(gain_sb, gain)
        load_table(2)
        load_w1(2)
        wgs_rows = wgs.rearrange("(q t) j -> q t j", t=PACK)
        wgs_sb = [sb([P, S], F32, f"wgs_sb{t}") for t in range(PACK)]
        page_rows = page0.rearrange("(p t) m -> p t m", t=PACK)
        page = [sb([P, T2], F32, f"page{t}") for t in range(PACK)]

        def load_wgs(t, cols):
            for q in (0, 2, 1, 3):
                nc.sync.dma_start(wgs_sb[t][32 * q : 32 * q + 32, cols], wgs_rows[:, t, cols])

        def load_slice(t):
            load_wgs(t, slice(0, S))
            nc.sync.dma_start(page[t][:], page_rows[:, t, :])

        load_wgs(0, half_cols[0])
        nc.sync.dma_start(page[0][:], page_rows[:, 0, :])
        load_wgs(0, half_cols[1])
        nc.sync.dma_start(idx3[:], offs3)
        load_vector(unit_sb, unit)
        load_vector(level_sb, level)
        w3_raw = sb([P, PACK, N], F32, "w3_raw")
        nc.sync.dma_start(w3_raw[:], w3.rearrange("(p j) n -> p j n", j=PACK))
        for t in range(1, PACK):
            load_slice(t)

        w2_c = sb([P, PASSES, 2 * H], U8, "w2_c")
        w2_s = sb([P, PASSES, H], U8, "w2_s")
        for a in range(PASSES):
            nc.vector.tensor_copy(
                w2_c[:, a, :].rearrange("p (t m b) -> p t m b", t=PACK, b=2),
                w2_raw[:, a, :].rearrange("p (m t b) -> p t m b", t=PACK, b=2),
            )
        nc.vector.tensor_copy(
            w2_s[:].rearrange("p a (t m) -> p a t m", t=PACK),
            w2_s_raw[:].rearrange("p a (m t) -> p a t m", t=PACK),
        )

        w1_c = sb([P, PASSES, H], U32, "w1_c")
        w1_s = sb([P, PASSES, H], U8, "w1_s")
        v_w = [sb([P, S], U32, f"v_w{a}") for a in range(PASSES)]
        for a in range(PASSES):
            w1_bf = sb([P, PACK * H], BF16, f"w1_bf{a}", tag=f"w1_bf{a % 2}")
            dealt = w1_bf[:].rearrange("p (t m j) -> p m j t", t=PACK, j=PACK)
            raw = w1_raw[a][:].rearrange("p j (m t) -> p m j t", t=PACK)
            for h in range(HALVES):
                nc.vector.tensor_copy(v_w[a][:, half_cols[h]], tab_w[a][:].bitcast(U32).indirect(idx[:, half_offs[h]]))
            if a < PASSES - 1:
                nc.scalar.activation(dealt, raw, ACT.Copy, scale=-1.0)
                spans = [(0, H)]
            else:
                nc.vector.tensor_scalar(dealt[:, :, :, 0], raw[:, :, :, 0], -1.0, None, MULT)
                nc.scalar.activation(dealt[:, :, :, 1:PACK], raw[:, :, :, 1:PACK], ACT.Copy, scale=-1.0)
                spans = [(0, P), (P, 2 * P), (2 * P, H)]
            for lo, hi in spans:
                nc.vector.quantize_mx(
                    out=w1_c[:, a, lo:hi].bitcast(FP8X4), scales=w1_s[:, a, lo:hi], in_=w1_bf[:, PACK * lo : PACK * hi]
                )

        hs = [sb([P, S], F32, f"hs{t}") for t in range(PACK)]
        for t in range(PACK):
            for h in range(HALVES):
                acc = psum.tile([P, BANK], F32, name=f"acc{t}{h}", tag=f"bank{t % 2}{h}")
                for a in range(PASSES):
                    rhs = v_w[a][:, half_cols[h]].bitcast(FP8X4)
                    rhs_scale = v_s[a][:, half_cols[h]]
                    nc.tensor.matmul_mx(
                        out=acc[:],
                        lhsT=w2_c[:, a, 2 * P * t : 2 * P * (t + 1)].bitcast(FP4X4),
                        lhsT_scale=w2_s[:, a, P * t : P * (t + 1)],
                        rhs=rhs, rhs_scale=rhs_scale, start=(a == 0), stop=False,
                    )
                    nc.tensor.matmul_mx(
                        out=acc[:],
                        lhsT=w1_c[:, a, P * t : P * (t + 1)].bitcast(FP8X4),
                        lhsT_scale=w1_s[:, a, P * t : P * (t + 1)],
                        rhs=rhs, rhs_scale=rhs_scale, start=False, stop=(a == PASSES - 1),
                    )
                nc.scalar.activation(hs[t][:, half_cols[h]], acc[:], ACT.Square)
            if t > 0:
                nc.scalar.activation(hs[t][:], hs[t][:], ACT.Copy, scale=gain_sb[:, t : t + 1])

        w3_bf = sb([P, N, PACK], BF16, "w3_bf")
        w3_s = sb([P, N], U8, "w3_s")
        nc.scalar.copy(w3_bf[:], w3_raw[:].rearrange("p j n -> p n j"))

        out1_rows = out_1.rearrange("(p t) m -> p t m", t=PACK)
        width = T2 // PLANE_CHUNKS
        chunk_cols = [slice(c * width, (c + 1) * width) for c in range(PLANE_CHUNKS)]
        rows4 = [
            sb([P, PACK, width], F32, f"rows4_{c}", tag=("big0", "big1", "rows4_2", "rows4_3")[c])
            for c in range(PLANE_CHUNKS)
        ]
        xg = sb([P, PACK, PM], F32, "xg", tag="big2")
        x_rows = [sb([P, PACK, BANK], BF16, f"x_rows{h}") for h in range(HALVES)]
        x_bf = [sb([P, BANK, PACK], BF16, f"x_bf{h}", tag=f"mid{h}") for h in range(HALVES)]
        size_last = sb([P, BANK], F32, "size_last")
        last = PACK - 1
        for t in range(PACK):
            if t == 0:
                for h in range(HALVES):
                    first = wgs_sb[0][:, half_cols[h]]
                    nc.vector.tensor_scalar(first, first, gain_sb[:, 0:1], None, MULT)
                    nc.vector.tensor_tensor(
                        page[t][:].indirect(idx2[:, half_offs[h]]), hs[t][:, half_cols[h]], first, MULT
                    )
            else:
                nc.vector.tensor_tensor(page[t][:].indirect(idx2[:]), hs[t][:], wgs_sb[t][:], MULT)
            for c in (3, 0, 1, 2):
                if t < last:
                    nc.scalar.copy(rows4[c][:, t, :], page[t][:, chunk_cols[c]])
                else:
                    nc.sync.dma_start(rows4[c][:, t, :], page[t][:, chunk_cols[c]])
            nc.sync.dma_start(out1_rows[:, t, :], page[t][:])
            pieces = [range(HALVES)] if t < last else [range(h, h + 1) for h in range(HALVES)]
            for halves in pieces:
                cols = slice(halves.start * BANK, halves.stop * BANK)
                cells = xg[:, t, cols]
                nc.vector.tensor_copy(cells, page[t][:].indirect(idx3[:, cols.start // 16 : cols.stop // 16]))
                size = cells if t < last else size_last[:]
                nc.scalar.activation(size, cells, ACT.Abs, scale=unit_sb[:, t : t + 1])
                nc.scalar.activation(cells, size, ACT.Ln, bias=1.0)
                for h in halves:
                    nc.scalar.activation(
                        x_rows[h][:, t, :], xg[:, t, half_cols[h]], ACT.Copy, scale=level_sb[:, t : t + 1]
                    )
        w3_c = sb([P, N], U32, "w3_c", tag="hs3")
        for lo, hi in ((0, 256), (256, N)):
            nc.vector.quantize_mx(
                out=w3_c[:, lo:hi].bitcast(FP8X4), scales=w3_s[:, lo:hi],
                in_=w3_bf[:, lo:hi, :].rearrange("p n j -> p (n j)"),
            )

        x_c = sb([P, PM], U32, "x_c")
        x_s = sb([P, PM], U8, "x_s")
        out0_rows = out_0.rearrange("(c p) m -> p c m", p=P)
        for h in range(HALVES):
            cols = half_cols[h]
            nc.vector.tensor_copy(x_bf[h][:], x_rows[h][:].rearrange("p t m -> p m t"))
            nc.vector.quantize_mx(
                out=x_c[:, cols].bitcast(FP8X4), scales=x_s[:, cols],
                in_=x_bf[h][:].rearrange("p m t -> p (m t)"),
            )
            y_sb = sb([P, N // P, BANK], F32, f"y_sb{h}", tag=("mid2", "w3_raw")[h])
            for c in range(N // P):
                y_ps = psum.tile([P, BANK], F32, name=f"y{c}{h}", tag=f"score{c}{h}" if c else f"bank0{h}")
                nc.tensor.matmul_mx(
                    out=y_ps[:],
                    lhsT=w3_c[:, P * c : P * (c + 1)].bitcast(FP8X4),
                    lhsT_scale=w3_s[:, P * c : P * (c + 1)],
                    rhs=x_c[:, cols].bitcast(FP8X4), rhs_scale=x_s[:, cols],
                    start=True, stop=True,
                )
                nc.scalar.copy(y_sb[:, c, :], y_ps[:])
                nc.sync.dma_start(out0_rows[:, c, cols], y_sb[:, c, :])

        p_s = sb([P, T2], U8, "p_s")
        words_out = out_2[0].rearrange("p m t -> p (m t)").bitcast(I32)
        for c in range(PLANE_CHUNKS):
            cols = chunk_cols[c]
            p_c = sb([P, width], I32, f"p_c{c}")
            page_bf = sb([P, width, PACK], BF16, f"page_bf{c}", tag=("x_rows0", "x_rows1", "mid1", "page_bf3")[c])
            if c < PLANE_CHUNKS - 1:
                nc.vector.tensor_copy(page_bf[:], rows4[c][:].rearrange("p t m -> p m t"))
            else:
                nc.scalar.copy(page_bf[:], rows4[c][:].rearrange("p t m -> p m t"))
            nc.vector.quantize_mx(
                out=p_c[:].bitcast(FP8X4), scales=p_s[:, cols],
                in_=page_bf[:].rearrange("p m t -> p (m t)"),
            )
            nc.sync.dma_start(words_out[:, cols], p_c[:])
        for q in range(QUADS):
            nc.sync.dma_start(out_3[0, 4 * q : 4 * q + 4, :].bitcast(I32), p_s[32 * q : 32 * q + 4, :].bitcast(I32))
